import numpy as np
import ml_dtypes


def mxq(x, axis, fmt="e4m3"):
    dtype, down = {"e4m3": (ml_dtypes.float8_e4m3fn, 7), "e5m2": (ml_dtypes.float8_e5m2, 14)}[fmt]
    v = np.moveaxis(np.asarray(x, np.float32).astype(ml_dtypes.bfloat16).astype(np.float64), axis, -1)
    blocks = v.reshape(v.shape[:-1] + (-1, 32))
    amax = np.abs(blocks).max(-1, keepdims=True)
    byte = np.maximum(np.where(amax > 0, np.frexp(amax)[1] - 1 + 127, 0) - down, 1)
    scale = np.exp2(byte - 127.0)
    codes = (blocks / scale).astype(np.float32).astype(dtype).astype(np.float64)
    return np.moveaxis((codes * scale).reshape(v.shape), -1, axis)


WIDE = False


def mx_kscale(k):
    if not WIDE:
        return np.ones(k)
    levels = np.array([10, -10, 5, -5, 0])
    if k % 512:
        return np.exp2(np.random.permutation(np.resize(levels, k // 32))).repeat(32)
    a = np.empty((k // 512, 16))
    for p in range(k // 512):
        a[p, :8] = np.random.permutation(np.resize(levels, 8))
        for g in range(8):
            far = levels[np.abs(levels - a[p, g]) >= 10]
            a[p, g + 8] = far[np.random.randint(len(far))]
    return np.exp2(a.ravel()).repeat(32)


BF16 = ml_dtypes.bfloat16


def bf(x):
    return np.asarray(x, np.float32).astype(BF16)


def f64(x):
    return np.asarray(x).astype(np.float64)


E2M1 = np.array([0.0, 0.5, 1.0, 1.5, 2.0, 3.0, 4.0, 6.0, -0.0, -0.5, -1.0, -1.5, -2.0, -3.0, -4.0, -6.0])


def pack_weight(w, fmt):
    k, n = w.shape
    w = f64(bf(w)).reshape(k // 32, 32, n)
    amax = np.abs(w).max(1)
    if fmt == "e4m3":
        byte = np.frexp(amax)[1] - 1 + 127 - 7
    else:
        mant, ex = np.frexp(amax / 6.0)
        byte = np.where(mant > 0.5, ex, ex - 1) + 127
    byte = np.clip(np.where(amax > 0, byte, 1), 1, 254)
    scaled = (w * np.exp2(127.0 - byte)[:, None, :]).reshape(k, n).astype(np.float32)
    by_word = np.ascontiguousarray(scaled.reshape(k // 512, 128, 4, n).transpose(0, 1, 3, 2))
    if fmt == "e4m3":
        words = by_word.astype(ml_dtypes.float8_e4m3fn).view(np.uint8)
    else:
        c = by_word.astype(ml_dtypes.float4_e2m1fn).view(np.uint8) & 0xF
        words = c[..., 0::2] | (c[..., 1::2] << 4)
    return np.ascontiguousarray(words), np.ascontiguousarray(byte.astype(np.uint8).reshape(k // 512, 16, n))


def unpack_weight(words, scales, fmt):
    g, p, n, _ = words.shape
    if fmt == "e4m3":
        vals = np.ascontiguousarray(words).view(ml_dtypes.float8_e4m3fn).astype(np.float64)
    else:
        nib = np.empty((g, p, n, 4), np.uint8)
        nib[..., 0::2] = words & 0xF
        nib[..., 1::2] = words >> 4
        vals = E2M1[nib]
    vals = vals * np.repeat(np.exp2(scales.astype(np.float64) - 127.0), 8, axis=1)[..., None]
    return vals.transpose(0, 1, 3, 2).reshape(g * 512, n)
def pack4(w):
    words, scales = pack_weight(w, "e2m1")
    return words.reshape(words.shape[0], 128, -1), scales


def unpack4(words, scales):
    return unpack_weight(words.reshape(words.shape[0], 128, -1, 2), scales, "e2m1")


E4M3FN = np.array([(-1.0 if i & 128 else 1.0) * ((1.0 + (i & 7) / 8.0) * 2.0 ** (((i >> 3) & 15) - 7) if i & 120 else (i & 7) * 2.0 ** -9) for i in range(256)])


def e4m3fn_bytes(y):
    return np.clip(np.asarray(y, np.float64), -448.0, 448.0).astype(np.float32).astype(ml_dtypes.float8_e4m3fn).view(np.uint8)


def e4m3fn_values(b):
    return E4M3FN[b]


B, N, M, D, F = 2, 512, 512, 512, 512


def erf(a):
    c = np.clip(a, -6.0, 6.0)
    c2 = 2.0 * c * c
    term = c.copy()
    total = c.copy()
    for n in range(1, 150):
        term *= c2
        term /= 2.0 * n + 1.0
        total += term
    r = 2.0 / np.sqrt(np.pi) * np.exp(-c * c) * total
    return np.where(np.abs(a) <= 6.0, r, np.sign(a))


def gelu_erf(t):
    return 0.5 * t * (1.0 + erf(t / np.sqrt(2.0)))


def draw0():
    s = mx_kscale(D)
    t = mx_kscale(M)
    x = bf(np.random.standard_normal((B, N, D)) * s)
    y = bf(np.random.standard_normal((B, M, D)) * 0.8 * s)
    g = bf((1.0 + 0.1 * np.random.standard_normal(D)) / (s * s))
    gp = bf(np.random.standard_normal(M) * t)
    gv = bf((1.0 + 0.1 * np.random.standard_normal(M)) / t)
    wr_words, wr_scales = pack4(np.random.standard_normal((D, F)) / np.sqrt(D) / s[:, None])
    wm_words, wm_scales = pack4(np.random.standard_normal((D, F)) * 3.0 / np.sqrt(D) / s[:, None])
    return {
        "x": x,
        "y": y,
        "g": g,
        "gp": gp,
        "gv": gv,
        "wr_words": wr_words,
        "wr_scales": wr_scales,
        "wm_words": wm_words,
        "wm_scales": wm_scales,
    }


def core(x, y, g, gp, gv, wr_words, wr_scales, wm_words, wm_scales):
    x, y, g, gp, gv = f64(x), f64(y), f64(g), f64(gp), f64(gv)

    yg = y * g[None, None, :]

    xq = mxq(x, 2, "e4m3")
    gram = xq @ mxq(yg, 2, "e4m3").transpose(0, 2, 1)

    sq = np.sum(yg * y, axis=-1)

    logits = (2.0 * gram - sq[:, None, :]) / np.sqrt(D)
    e = np.exp(logits - logits.max(-1, keepdims=True))
    p = e / e.sum(-1, keepdims=True)

    pg = p * gp[None, None, :]

    v = (mxq(y, 2, "e4m3") @ unpack4(wm_words, wm_scales)) * gv[None, :, None]

    u = (xq @ unpack4(wr_words, wr_scales)) + (mxq(pg, 2, "e4m3") @ mxq(v, 1, "e4m3"))

    return gelu_erf(u)


def setup_inputs():
    drawn = draw0()
    full = np.asarray(drawn['x']).astype(np.float64)
    scale = (np.abs(full).reshape(2, 512, 4, 128).max(axis=(3,)) / 448.0).astype(np.float32)
    given = {}
    for key, value in drawn.items():
        if key == 'x':
            given['x_bytes'] = e4m3fn_bytes(full / np.repeat(scale.astype(np.float64), 128, axis=2))
            given['x_scale'] = scale
        else:
            given[key] = value
    return given


def reference(x_bytes, x_scale, y, g, gp, gv, wr_words, wr_scales, wm_words, wm_scales):
    return core(e4m3fn_values(x_bytes) * np.repeat(x_scale.astype(np.float64), 128, axis=2), y, g, gp, gv, wr_words, wr_scales, wm_words, wm_scales)

@@ -1,0 +1,452 @@
+from contextlib import ExitStack
+
+import concourse.mybir as mybir
+from concourse.masks import make_identity
+
+B, N, M, D, F = 2, 512, 512, 512, 512
+FLOPS = 4 * 2 * B * 512 * 512 * 512
+
+F32 = mybir.dt.float32
+BF16 = mybir.dt.bfloat16
+U32 = mybir.dt.uint32
+I32 = mybir.dt.int32
+U8 = mybir.dt.uint8
+E4M3 = mybir.dt.float8_e4m3fn
+E4M3X4 = mybir.dt.float8_e4m3fn_x4
+E2M1X4 = mybir.dt.float4_e2m1fn_x4
+ACT = mybir.ActivationFunctionType
+ALU = mybir.AluOpType
+AX = mybir.AxisListType
+
+P = 128
+RSD = 512 ** -0.5
+
+
+def tile_visiongnnsoftgrapher_d1p_kernel(
+    tc, x_bytes, x_scale, y, g, gp, gv, wr_words, wr_scales, wm_words, wm_scales, out
+):
+    nc = tc.nc
+    with ExitStack() as ctx:
+        pool = ctx.enter_context(tc.tile_pool(name="sb", bufs=1))
+        psum = ctx.enter_context(tc.psum_pool(name="ps", bufs=1))
+        ctx.enter_context(tc.manual_schedule())
+
+        def sb(name, shape, dt):
+            return pool.tile(shape, dt, name=name, tag=name, bufs=1, align_bytes=64)
+
+        def bank(tag, bufs):
+            return psum.tile([P, 512], F32, name=tag, tag=tag, bufs=bufs)
+
+        def tbank():
+            return bank("tp", 2)
+
+        def mbank():
+            return bank("mm", 5)
+
+        xs = sb("xs", [P, B, 16], F32)
+        nc.sync.dma_start(out=xs[:], in_=x_scale.rearrange("b (p i) q -> p b (i q)", i=4))
+        x8 = [sb("x8_%d" % b, [P, 2048], U8) for b in range(B)]
+        ysb = [[sb("y_%d_%d" % (b, v), [P, 2, 512], BF16) for v in range(2)] for b in range(B)]
+        y_v = [y[b].rearrange("(p t) d -> p t d", t=4) for b in range(B)]
+        x_v = [x_bytes[b].rearrange("(p i) d -> p (i d)", i=4) for b in range(B)]
+        small = {}
+
+        def load_small(nm, src):
+            small[nm] = sb("s_" + nm, [P, 4], BF16)
+            nc.sync.dma_start(out=small[nm][:], in_=src.rearrange("(p t) -> p t", t=4))
+
+        def load_y(b):
+            for v in range(2):
+                nc.sync.dma_start(out=ysb[b][v][:], in_=y_v[b][:, 2 * v : 2 * v + 2, :])
+
+        wq = {}
+        ws = {}
+        for nm in ("wm", "wr"):
+            wq[nm] = sb("w_" + nm, [P, 1024], U8)
+            ws[nm] = sb("ws_" + nm, [P, 512], U8)
+            nc.vector.memset(ws[nm][:].bitcast(I32), 0)
+
+        def load_w(nm, w, s):
+            nc.sync.dma_start(out=wq[nm][:], in_=w[0])
+            for q in range(4):
+                nc.sync.dma_start(
+                    out=ws[nm][32 * q : 32 * q + 4, :].bitcast(I32), in_=s[0, 4 * q : 4 * q + 4, :].bitcast(I32)
+                )
+
+        nc.sync.dma_start(out=x8[0][:], in_=x_v[0])
+        load_y(0)
+        load_small("g", g)
+        nc.sync.dma_start(out=x8[1][:], in_=x_v[1])
+        load_y(1)
+        load_small("gv", gv)
+        load_w("wm", wm_words, wm_scales)
+        load_small("gp", gp)
+        load_w("wr", wr_words, wr_scales)
+
+        ident = sb("ident", [P, P], F32)
+        make_identity(nc, ident[:])
+        warm = sb("warm", [P, 2], F32)
+        nc.vector.memset(warm[:], 0.0)
+        nc.scalar.activation(out=warm[:, 1:2], in_=warm[:, 0:1], func=ACT.Exp)
+        gl = sb("gl", [P, 4, P], F32)
+        nc.gpsimd.tensor_copy(out=gl[:], in_=small["g"][:].unsqueeze(2).to_broadcast([P, 4, P]))
+        gv32 = sb("gv32", [P, 4], F32)
+        nc.gpsimd.tensor_copy(out=gv32[:], in_=small["gv"][:])
+        gp32 = sb("gp32", [P, 4], F32)
+        nc.gpsimd.tensor_copy(out=gp32[:], in_=small["gp"][:])
+
+        xb = [sb("xb_%d" % b, [P, 4, 512], BF16) for b in range(B)]
+        xT = [sb("xT_%d" % b, [P, 512, 4], BF16) for b in range(B)]
+        yT = [sb("yT_%d" % b, [P, 4, P, 4], BF16) for b in range(B)]
+        ygT = [sb("ygT_%d" % b, [P, 2, P, 2, 4], BF16) for b in range(B)]
+        y2 = [sb("y2_%d" % b, [P, 4, 2, P, 2], F32) for b in range(B)]
+        sqs = [sb("sqs_%d" % b, [P, 512], F32) for b in range(B)]
+        gpb = sb("gpb", [P, 2, P, 2], BF16)
+        vb = [sb("vb_%d" % b, [P, 4, 512], BF16) for b in range(B)]
+        vT = [sb("vT_%d" % b, [P, 512, 4], BF16) for b in range(B)]
+        codes = {}
+        for nm in ("x", "y", "yg", "v", "pg"):
+            for b in range(B):
+                codes[nm, b] = (sb("c_%s_%d" % (nm, b), [P, 512], U32), sb("k_%s_%d" % (nm, b), [P, 512], U8))
+
+        def quant(nm, b, lo, hi, flat):
+            c, k = codes[nm, b]
+            nc.vector.quantize_mx(out=c[:, lo:hi].bitcast(E4M3X4), scales=k[:, lo:hi], in_=flat)
+
+        def widen(b, i, q, eng):
+            o = xb[b][:, i, 128 * q : 128 * q + 128]
+            s = xs[:, b, 4 * i + q : 4 * i + q + 1]
+            src8 = x8[b][:, 512 * i + 128 * q : 512 * i + 128 * q + 128].bitcast(E4M3)
+            if eng == "v":
+                nc.vector.tensor_scalar(out=o, in0=src8, scalar1=s, scalar2=None, op0=ALU.mult)
+            else:
+                nc.scalar.activation(out=o, in_=src8, func=ACT.Copy, scale=s)
+
+        def trans_pair(rows0, rows1):
+            tb = tbank()
+            t4 = tb[:].rearrange("p (e u r) -> p e u r", e=2, u=2)
+            for e, rows in ((0, rows0), (1, rows1)):
+                w = rows.bitcast(F32)
+                for u in range(2):
+                    nc.tensor.transpose(t4[:, e, u, :], w[:, u:256:2], ident[:])
+            return t4
+
+        def evac(eng, dst_words, t4):
+            src_v = t4.rearrange("p e u r -> p e r u")
+            if eng == "v":
+                nc.vector.tensor_copy(out=dst_words, in_=src_v)
+            else:
+                nc.scalar.copy(out=dst_words, in_=src_v)
+
+        tps = {}
+
+        def y_tp(b, v):
+            tps["y", b, v] = trans_pair(ysb[b][v][:, 0, :], ysb[b][v][:, 1, :])
+
+        def y_ev(b, v, eng):
+            dst = yT[b][:, 2 * v : 2 * v + 2, :, :].rearrange("p t r k -> p (t r k)").bitcast(F32)
+            evac(eng, dst.rearrange("p (e r u) -> p e r u", e=2, u=2), tps["y", b, v])
+
+        def x_tp(b, v):
+            tps["x", b, v] = trans_pair(xb[b][:, 2 * v, :], xb[b][:, 2 * v + 1, :])
+
+        def x_ev(b, v, eng):
+            dst = xT[b][:, 256 * v : 256 * v + 256, :].rearrange("p r k -> p (r k)").bitcast(F32)
+            evac(eng, dst.rearrange("p (e r u) -> p e r u", e=2, u=2), tps["x", b, v])
+
+        def yg_mul(b, v):
+            nc.vector.tensor_tensor(
+                out=ygT[b][:, v],
+                in0=yT[b][:, 2 * v : 2 * v + 2, :, :].rearrange("p e r k -> p r e k"),
+                in1=small["g"][:].unsqueeze(1).unsqueeze(1).to_broadcast([P, P, 2, 4]),
+                op=ALU.mult,
+            )
+
+        def quant_yg(b, v):
+            quant("yg", b, 256 * v, 256 * v + 256, ygT[b][:, v].rearrange("p r e k -> p (r e k)"))
+
+        def quant_y(b, v):
+            quant("y", b, 256 * v, 256 * v + 256, yT[b][:, 2 * v : 2 * v + 2].rearrange("p t r k -> p (t r k)"))
+
+        def quant_x(b, v):
+            quant("x", b, 256 * v, 256 * v + 256, xT[b][:, 256 * v : 256 * v + 256].rearrange("p r k -> p (r k)"))
+
+        def square(b, v):
+            nc.scalar.activation(
+                out=y2[b][:, :, v],
+                in_=yT[b][:, 2 * v : 2 * v + 2, :, :].rearrange("p e r k -> p k r e"),
+                func=ACT.Square,
+            )
+
+        sq_ps = {}
+
+        def sq_mm(b, v):
+            if v == 0:
+                sq_ps[b] = bank("sq", 1)
+            for k in range(4):
+                nc.tensor.matmul(
+                    sq_ps[b][:, 256 * v : 256 * v + 256],
+                    lhsT=gl[:, k, :],
+                    rhs=y2[b][:, k, v].rearrange("p r e -> p (r e)"),
+                    start=(k == 0),
+                    stop=(k == 3),
+                )
+
+        def sq_copy(b):
+            nc.scalar.activation(out=sqs[b][:], in_=sq_ps[b][:], func=ACT.Copy, scale=RSD)
+
+        def mx(o, a, asl, wt, start, stop):
+            ca, ka = a
+            nc.tensor.matmul_mx(
+                out=o,
+                lhsT=ca[:, asl].bitcast(E4M3X4),
+                lhsT_scale=ka[:, asl],
+                rhs=wt[0],
+                rhs_scale=wt[1],
+                start=start,
+                stop=stop,
+            )
+
+        def cols(i):
+            return slice(128 * i, 128 * i + 128)
+
+        def mov(nm, b):
+            c, k = codes[nm, b]
+            return c[:].bitcast(E4M3X4), k[:]
+
+        def wmov(nm, lo, n):
+            return wq[nm][:, 2 * lo : 2 * lo + 2 * n].bitcast(E2M1X4), ws[nm][:, lo : lo + n]
+
+        v_ps = {}
+
+        def v_mm(b, t):
+            v_ps[b, t] = mbank()
+            mx(v_ps[b, t][:], codes["y", b], cols(t), wmov("wm", 0, 512), True, True)
+
+        def v_sc(b, t):
+            nc.scalar.activation(out=vb[b][:, t, :], in_=v_ps[b, t][:], func=ACT.Copy, scale=gv32[:, t : t + 1])
+
+        def v_inter(b, h):
+            nc.vector.tensor_copy(
+                out=vT[b][:, 256 * h : 256 * h + 256, :], in_=vb[b][:, :, 256 * h : 256 * h + 256].rearrange("p t f -> p f t")
+            )
+
+        def v_mm4(b, c):
+            v_ps[b, c] = mbank()
+            for t in range(4):
+                mx(v_ps[b, c][:, 128 * t : 128 * t + 128], codes["y", b], cols(t), wmov("wm", 128 * c, 128), True, True)
+
+        def v_mul(b, c):
+            nc.vector.tensor_tensor(
+                out=vT[b][:, 128 * c : 128 * c + 128, :],
+                in0=v_ps[b, c][:].rearrange("p (t f) -> p f t", t=4),
+                in1=gv32[:].unsqueeze(1).to_broadcast([P, P, 4]),
+                op=ALU.mult,
+            )
+
+        def quant_v(b, h):
+            quant("v", b, 256 * h, 256 * h + 256, vT[b][:, 256 * h : 256 * h + 256].rearrange("p f t -> p (f t)"))
+
+        def gp_tp():
+            tps["gp"] = tbank()
+            for t in range(4):
+                nc.tensor.transpose(tps["gp"][:, 128 * t : 128 * t + 128], gp32[:, t : t + 1].to_broadcast([P, P]), ident[:])
+
+        def gp_ev():
+            nc.scalar.copy(out=gpb[:], in_=tps["gp"][:].rearrange("p (u e r) -> p u r e", u=2, e=2))
+
+        nl = {}
+        ex = {}
+        mn = {}
+        zs = {}
+        rz = {}
+        gram_ps = {}
+
+        def gram(b, i):
+            ps = mbank()
+            mx(ps[:], codes["x", b], cols(i), mov("yg", b), True, True)
+            gram_ps[b, i] = ps
+
+        def logit(b, i):
+            nl[b, i] = sb("nl_%d_%d" % (b, i), [P, 512], F32)
+            nc.vector.scalar_tensor_tensor(
+                out=nl[b, i][:], in0=gram_ps[b, i][:], scalar=-2.0 * RSD, in1=sqs[b][:], op0=ALU.mult, op1=ALU.add
+            )
+
+        def rmin(b, i):
+            mn[b, i] = sb("mn_%d_%d" % (b, i), [P, 1], F32)
+            nc.vector.tensor_reduce(out=mn[b, i][:], in_=nl[b, i][:], axis=AX.X, op=ALU.min)
+
+        def exp(b, i):
+            ex[b, i] = sb("ex_%d_%d" % (b, i), [P, 512], F32)
+            zs[b, i] = sb("zs_%d_%d" % (b, i), [P, 1], F32)
+            nc.scalar.activation(
+                out=ex[b, i][:], in_=nl[b, i][:], func=ACT.Exp, bias=mn[b, i][:], scale=-1.0, accum_out=zs[b, i][:]
+            )
+
+        def recip(b, i):
+            rz[b, i] = sb("rz_%d_%d" % (b, i), [P, 1], F32)
+            nc.vector.reciprocal(out=rz[b, i][:], in_=zs[b, i][:])
+
+        pgs = {}
+
+        def pg_mul(b, i):
+            pgs[b, i] = sb("pg_%d_%d" % (b, i), [P, 512], BF16)
+            nc.vector.scalar_tensor_tensor(
+                out=pgs[b, i][:],
+                in0=ex[b, i][:],
+                scalar=rz[b, i][:],
+                in1=gpb[:].rearrange("p u r e -> p (u r e)"),
+                op0=ALU.mult,
+                op1=ALU.mult,
+            )
+
+        pgT = {}
+
+        def pg_tp(b, i):
+            tb = tbank()
+            tps["pg", b, i] = tb
+            w = pgs[b, i][:].bitcast(F32)
+            for u in range(2):
+                nc.tensor.transpose(tb[:, 128 * u : 128 * u + 128], w[:, 128 * u : 128 * u + 128], ident[:])
+
+        def pg_ev(b, i, eng):
+            pgT[b, i] = sb("pgT_%d_%d" % (b, i), [P, 512], BF16)
+            dst = pgT[b, i][:].bitcast(F32).rearrange("p (r u) -> p r u", u=2)
+            src_v = tps["pg", b, i][:, 0:256].rearrange("p (u r) -> p r u", u=2)
+            if eng == "v":
+                nc.vector.tensor_copy(out=dst, in_=src_v)
+            else:
+                nc.scalar.copy(out=dst, in_=src_v)
+
+        def quant_pg(b, i):
+            quant("pg", b, 128 * i, 128 * i + 128, pgT[b, i][:])
+
+        u_ps = {}
+
+        def u_mx(b, i):
+            u_ps[b, i] = mbank()
+            mx(u_ps[b, i][:], codes["x", b], cols(i), wmov("wr", 0, 512), True, False)
+
+        def u_mp(b, i):
+            mx(u_ps[b, i][:], codes["pg", b], cols(i), mov("v", b), False, True)
+
+        def gelu_warm():
+            nc.scalar.activation(out=warm[:, 1:2], in_=warm[:, 0:1], func=ACT.Gelu)
+
+        o_v = [out[b].rearrange("(p i) f -> p i f", i=4) for b in range(B)]
+
+        def finish(b, i):
+            o = sb("o_%d_%d" % (b, i), [P, 512], F32)
+            nc.scalar.activation(out=o[:], in_=u_ps[b, i][:], func=ACT.Gelu)
+            nc.sync.dma_start(out=o_v[b][:, i, :], in_=o[:])
+
+        def both(f, *a):
+            f(*a, 0)
+            f(*a, 1)
+
+        for i in range(4):
+            for q in range(4):
+                widen(0, i, q, "s" if i == 3 else "v")
+        for v in range(2):
+            y_tp(0, v)
+            y_ev(0, v, "s")
+        for v in range(2):
+            x_tp(0, v)
+            x_ev(0, v, "s")
+        for i in range(2):
+            for q in range(4):
+                widen(1, i, q, "v")
+        both(yg_mul, 0)
+        both(quant_yg, 0)
+        both(quant_y, 0)
+        square(0, 0)
+        for v in range(2):
+            y_tp(1, v)
+            y_ev(1, v, "s")
+        square(0, 1)
+        both(quant_x, 0)
+        for i in range(2, 4):
+            for q in range(4):
+                widen(1, i, q, "v")
+        sq_mm(0, 0)
+        for c in range(4):
+            v_mm4(0, c)
+        both(yg_mul, 1)
+        both(quant_yg, 1)
+        both(quant_y, 1)
+        x_tp(1, 0)
+        x_ev(1, 0, "s")
+        sq_mm(0, 1)
+        x_tp(1, 1)
+        square(1, 0)
+        sq_copy(0)
+        x_ev(1, 1, "s")
+        square(1, 1)
+        for c in range(4):
+            v_mul(0, c)
+            if c == 2:
+                quant_v(0, 0)
+        gp_tp()
+        gp_ev()
+        gram(0, 0)
+        gram(0, 1)
+        v_mm(1, 0)
+        logit(0, 0)
+        quant_v(0, 1)
+        v_sc(1, 0)
+        gram(0, 2)
+        sq_mm(1, 0)
+        logit(0, 1)
+        rmin(0, 0)
+        exp(0, 0)
+        v_mm(1, 1)
+        v_sc(1, 1)
+        gram(0, 3)
+        logit(0, 2)
+        rmin(0, 1)
+        exp(0, 1)
+        v_mm(1, 2)
+        v_sc(1, 2)
+        sq_mm(1, 1)
+        logit(0, 3)
+        rmin(0, 2)
+        exp(0, 2)
+        v_mm(1, 3)
+        v_sc(1, 3)
+        rmin(0, 3)
+        exp(0, 3)
+        sq_copy(1)
+        both(quant_x, 1)
+        gram(1, 0)
+        gram(1, 1)
+        v_inter(1, 0)
+        v_inter(1, 1)
+        both(quant_v, 1)
+        logit(1, 0)
+        logit(1, 1)
+        gram(1, 2)
+        gram(1, 3)
+        for i in range(4):
+            if 0 < i < 3:
+                logit(1, i + 1)
+            rmin(1, i)
+            exp(1, i)
+            recip(0, i)
+        gelu_warm()
+        tiles = [(b, i) for b in range(B) for i in range(4)]
+        n = len(tiles)
+        for s in range(n + 5):
+            if s < n:
+                pg_mul(*tiles[s])
+                pg_tp(*tiles[s])
+            if 1 <= s < n + 1:
+                pg_ev(*tiles[s - 1], "v" if s - 1 in (0, 1, 2) else "s")
+            if 2 <= s < 6:
+                recip(1, s - 2)
+            if 2 <= s < n + 2:
+                quant_pg(*tiles[s - 2])
+                u_mx(*tiles[s - 2])
+                u_mp(*tiles[s - 2])
+            if 3 <= s < n + 3:
+                finish(*tiles[s - 3])

@@ -38,10 +38,10 @@ def tile_visiongnnsoftgrapher_d1p_kernel(
             return psum.tile([P, 512], F32, name=tag, tag=tag, bufs=bufs)
 
         def tbank():
-            return bank("tp", 2)
+            return bank("tp", 3)
 
         def mbank():
-            return bank("mm", 5)
+            return bank("mm", 4)
 
         xs = sb("xs", [P, B, 16], F32)
         nc.sync.dma_start(out=xs[:], in_=x_scale.rearrange("b (p i) q -> p b (i q)", i=4))
@@ -55,9 +55,8 @@ def tile_visiongnnsoftgrapher_d1p_kernel(
             small[nm] = sb("s_" + nm, [P, 4], BF16)
             nc.sync.dma_start(out=small[nm][:], in_=src.rearrange("(p t) -> p t", t=4))
 
-        def load_y(b):
-            for v in range(2):
-                nc.sync.dma_start(out=ysb[b][v][:], in_=y_v[b][:, 2 * v : 2 * v + 2, :])
+        def load_y(b, v):
+            nc.sync.dma_start(out=ysb[b][v][:], in_=y_v[b][:, 2 * v : 2 * v + 2, :])
 
         wq = {}
         ws = {}
@@ -73,11 +72,14 @@ def tile_visiongnnsoftgrapher_d1p_kernel(
                     out=ws[nm][32 * q : 32 * q + 4, :].bitcast(I32), in_=s[0, 4 * q : 4 * q + 4, :].bitcast(I32)
                 )
 
-        nc.sync.dma_start(out=x8[0][:], in_=x_v[0])
-        load_y(0)
-        load_small("g", g)
+        nc.sync.dma_start(out=x8[0][:, 0:1024], in_=x_v[0][:, 0:1024])
+        nc.sync.dma_start(out=x8[0][:, 1024:2048], in_=x_v[0][:, 1024:2048])
+        load_y(0, 0)
         nc.sync.dma_start(out=x8[1][:], in_=x_v[1])
-        load_y(1)
+        load_y(0, 1)
+        load_small("g", g)
+        load_y(1, 0)
+        load_y(1, 1)
         load_small("gv", gv)
         load_w("wm", wm_words, wm_scales)
         load_small("gp", gp)
@@ -113,14 +115,15 @@ def tile_visiongnnsoftgrapher_d1p_kernel(
             c, k = codes[nm, b]
             nc.vector.quantize_mx(out=c[:, lo:hi].bitcast(E4M3X4), scales=k[:, lo:hi], in_=flat)
 
-        def widen(b, i, q, eng):
-            o = xb[b][:, i, 128 * q : 128 * q + 128]
-            s = xs[:, b, 4 * i + q : 4 * i + q + 1]
-            src8 = x8[b][:, 512 * i + 128 * q : 512 * i + 128 * q + 128].bitcast(E4M3)
-            if eng == "v":
-                nc.vector.tensor_scalar(out=o, in0=src8, scalar1=s, scalar2=None, op0=ALU.mult)
-            else:
-                nc.scalar.activation(out=o, in_=src8, func=ACT.Copy, scale=s)
+        def widen(b, i, eng):
+            for q in range(4):
+                o = xb[b][:, i, 128 * q : 128 * q + 128]
+                s = xs[:, b, 4 * i + q : 4 * i + q + 1]
+                src8 = x8[b][:, 512 * i + 128 * q : 512 * i + 128 * q + 128].bitcast(E4M3)
+                if eng == "v":
+                    nc.vector.tensor_scalar(out=o, in0=src8, scalar1=s, scalar2=None, op0=ALU.mult)
+                else:
+                    nc.scalar.activation(out=o, in_=src8, func=ACT.Copy, scale=s)
 
         def trans_pair(rows0, rows1):
             tb = tbank()
@@ -338,115 +341,182 @@ def tile_visiongnnsoftgrapher_d1p_kernel(
 
         def finish(b, i):
             o = sb("o_%d_%d" % (b, i), [P, 512], F32)
-            nc.scalar.activation(out=o[:], in_=u_ps[b, i][:], func=ACT.Gelu)
-            nc.sync.dma_start(out=o_v[b][:, i, :], in_=o[:])
+            parts = 2 if (b, i) == (B - 1, 3) else 1
+            w = 512 // parts
+            for h in range(parts):
+                nc.scalar.activation(out=o[:, h * w : h * w + w], in_=u_ps[b, i][:, h * w : h * w + w], func=ACT.Gelu)
+                nc.sync.dma_start(out=o_v[b][:, i, h * w : h * w + w], in_=o[:, h * w : h * w + w])
 
-        def both(f, *a):
-            f(*a, 0)
-            f(*a, 1)
-
-        for i in range(4):
-            for q in range(4):
-                widen(0, i, q, "s" if i == 3 else "v")
-        for v in range(2):
-            y_tp(0, v)
-            y_ev(0, v, "s")
-        for v in range(2):
-            x_tp(0, v)
-            x_ev(0, v, "s")
-        for i in range(2):
-            for q in range(4):
-                widen(1, i, q, "v")
-        both(yg_mul, 0)
-        both(quant_yg, 0)
-        both(quant_y, 0)
+        widen(0, 0, "v")
+        widen(0, 1, "s")
+        widen(0, 2, "v")
+        x_tp(0, 0)
+        widen(1, 0, "s")
+        y_tp(0, 0)
+        y_tp(0, 1)
+        y_ev(0, 0, "s")
+        widen(0, 3, "v")
+        x_ev(0, 0, "v")
+        quant_x(0, 0)
+        y_tp(1, 0)
+        widen(1, 1, "v")
+        y_tp(1, 1)
+        quant_y(0, 0)
+        y_ev(0, 1, "s")
+        y_ev(1, 0, "v")
+        quant_y(0, 1)
+        x_tp(0, 1)
+        yg_mul(0, 0)
         square(0, 0)
-        for v in range(2):
-            y_tp(1, v)
-            y_ev(1, v, "s")
-        square(0, 1)
-        both(quant_x, 0)
-        for i in range(2, 4):
-            for q in range(4):
-                widen(1, i, q, "v")
-        sq_mm(0, 0)
-        for c in range(4):
-            v_mm4(0, c)
-        both(yg_mul, 1)
-        both(quant_yg, 1)
-        both(quant_y, 1)
+        yg_mul(0, 1)
         x_tp(1, 0)
-        x_ev(1, 0, "s")
+        square(0, 1)
+        v_mm(0, 0)
+        yg_mul(1, 0)
+        quant_yg(0, 0)
+        x_ev(0, 1, "s")
+        v_mm(0, 1)
+        v_mm(0, 2)
+        v_mm(0, 3)
+        y_ev(1, 1, "s")
+        widen(1, 2, "v")
+        x_ev(1, 0, "v")
+        sq_mm(0, 0)
+        v_sc(0, 0)
+        quant_yg(0, 1)
+        v_sc(0, 1)
+        v_sc(0, 2)
+        quant_y(1, 0)
+        quant_yg(1, 0)
+        v_sc(0, 3)
+        quant_x(0, 1)
         sq_mm(0, 1)
-        x_tp(1, 1)
-        square(1, 0)
-        sq_copy(0)
-        x_ev(1, 1, "s")
-        square(1, 1)
-        for c in range(4):
-            v_mul(0, c)
-            if c == 2:
-                quant_v(0, 0)
-        gp_tp()
-        gp_ev()
+        yg_mul(1, 1)
         gram(0, 0)
         gram(0, 1)
-        v_mm(1, 0)
-        logit(0, 0)
-        quant_v(0, 1)
-        v_sc(1, 0)
         gram(0, 2)
+        widen(1, 3, "s")
+        gram(0, 3)
+        quant_y(1, 1)
+        quant_x(1, 0)
+        gp_tp()
+        x_tp(1, 1)
+        v_inter(0, 0)
+        v_inter(0, 1)
+        quant_v(0, 0)
+        square(1, 0)
+        quant_v(0, 1)
+        sq_copy(0)
         sq_mm(1, 0)
+        square(1, 1)
+        gp_ev()
+        quant_yg(1, 1)
+        logit(0, 0)
         logit(0, 1)
         rmin(0, 0)
-        exp(0, 0)
-        v_mm(1, 1)
-        v_sc(1, 1)
-        gram(0, 3)
+        v_mm(1, 0)
+        sq_mm(1, 1)
         logit(0, 2)
+        x_ev(1, 1, "s")
+        v_mm(1, 1)
+        exp(0, 0)
         rmin(0, 1)
         exp(0, 1)
-        v_mm(1, 2)
-        v_sc(1, 2)
-        sq_mm(1, 1)
         logit(0, 3)
+        recip(0, 0)
         rmin(0, 2)
-        exp(0, 2)
-        v_mm(1, 3)
-        v_sc(1, 3)
+        v_mm(1, 2)
         rmin(0, 3)
+        v_sc(1, 0)
+        exp(0, 2)
+        recip(0, 1)
         exp(0, 3)
-        sq_copy(1)
-        both(quant_x, 1)
+        pg_mul(0, 0)
         gram(1, 0)
         gram(1, 1)
-        v_inter(1, 0)
-        v_inter(1, 1)
-        both(quant_v, 1)
-        logit(1, 0)
-        logit(1, 1)
+        quant_x(1, 1)
+        recip(0, 2)
+        sq_copy(1)
+        v_sc(1, 1)
+        pg_mul(0, 1)
+        v_sc(1, 2)
+        pg_mul(0, 2)
+        pg_tp(0, 0)
+        recip(0, 3)
+        pg_tp(0, 1)
         gram(1, 2)
+        logit(1, 0)
         gram(1, 3)
-        for i in range(4):
-            if 0 < i < 3:
-                logit(1, i + 1)
-            rmin(1, i)
-            exp(1, i)
-            recip(0, i)
+        logit(1, 1)
+        rmin(1, 0)
+        rmin(1, 1)
+        logit(1, 2)
+        pg_ev(0, 0, "s")
+        pg_ev(0, 1, "s")
+        pg_tp(0, 2)
+        quant_pg(0, 0)
+        v_mm(1, 3)
+        exp(1, 0)
+        u_mx(0, 0)
+        v_sc(1, 3)
+        logit(1, 3)
+        u_mx(0, 1)
+        rmin(1, 2)
+        recip(1, 0)
+        exp(1, 1)
+        rmin(1, 3)
+        pg_ev(0, 2, "s")
+        quant_pg(0, 1)
+        exp(1, 2)
+        recip(1, 1)
+        pg_mul(0, 3)
+        u_mp(0, 0)
+        pg_mul(1, 0)
+        recip(1, 2)
+        exp(1, 3)
+        pg_mul(1, 1)
+        u_mx(0, 2)
+        u_mx(1, 0)
+        pg_tp(1, 0)
+        u_mp(0, 1)
+        pg_tp(1, 1)
+        finish(0, 0)
+        pg_mul(1, 2)
+        v_inter(1, 0)
+        pg_ev(1, 0, "s")
+        v_inter(1, 1)
+        pg_ev(1, 1, "s")
+        finish(0, 1)
+        quant_pg(0, 2)
+        quant_v(1, 0)
+        pg_tp(0, 3)
+        pg_tp(1, 2)
+        quant_pg(1, 0)
+        pg_ev(0, 3, "s")
+        recip(1, 3)
+        u_mx(1, 1)
+        quant_v(1, 1)
+        pg_ev(1, 2, "s")
+        quant_pg(1, 1)
+        u_mp(0, 2)
+        u_mx(1, 2)
+        pg_mul(1, 3)
         gelu_warm()
-        tiles = [(b, i) for b in range(B) for i in range(4)]
-        n = len(tiles)
-        for s in range(n + 5):
-            if s < n:
-                pg_mul(*tiles[s])
-                pg_tp(*tiles[s])
-            if 1 <= s < n + 1:
-                pg_ev(*tiles[s - 1], "v" if s - 1 in (0, 1, 2) else "s")
-            if 2 <= s < 6:
-                recip(1, s - 2)
-            if 2 <= s < n + 2:
-                quant_pg(*tiles[s - 2])
-                u_mx(*tiles[s - 2])
-                u_mp(*tiles[s - 2])
-            if 3 <= s < n + 3:
-                finish(*tiles[s - 3])
+        u_mp(1, 0)
+        u_mp(1, 1)
+        pg_tp(1, 3)
+        quant_pg(1, 2)
+        quant_pg(0, 3)
+        pg_ev(1, 3, "v")
+        finish(0, 2)
+        u_mp(1, 2)
+        u_mx(0, 3)
+        quant_pg(1, 3)
+        finish(1, 0)
+        u_mp(0, 3)
+        u_mx(1, 3)
+        finish(1, 1)
+        finish(1, 2)
+        finish(0, 3)
+        u_mp(1, 3)
+        finish(1, 3)

@@ -85,6 +85,13 @@ def tile_visiongnnsoftgrapher_d1p_kernel(
         load_small("gp", gp)
         load_w("wr", wr_words, wr_scales)
 
+        zz = sb("zz", [P, P], F32)
+        nc.vector.memset(zz[:], 0.0)
+        wps = bank("sq", 1)
+
+        def warm_pe(b, k):
+            nc.tensor.matmul(wps[:, 0:128], lhsT=zz[:], rhs=zz[:], start=True, stop=True)
+
         ident = sb("ident", [P, P], F32)
         make_identity(nc, ident[:])
         warm = sb("warm", [P, 2], F32)
@@ -347,176 +354,188 @@ def tile_visiongnnsoftgrapher_d1p_kernel(
                 nc.scalar.activation(out=o[:, h * w : h * w + w], in_=u_ps[b, i][:, h * w : h * w + w], func=ACT.Gelu)
                 nc.sync.dma_start(out=o_v[b][:, i, h * w : h * w + w], in_=o[:, h * w : h * w + w])
 
-        widen(0, 0, "v")
-        widen(0, 1, "s")
-        widen(0, 2, "v")
-        x_tp(0, 0)
+        warm_pe(0, 0)
+        warm_pe(0, 1)
+        warm_pe(0, 2)
         widen(1, 0, "s")
-        y_tp(0, 0)
-        y_tp(0, 1)
-        y_ev(0, 0, "s")
+        warm_pe(0, 3)
+        warm_pe(0, 4)
+        warm_pe(0, 5)
+        widen(0, 0, "v")
+        warm_pe(0, 6)
+        warm_pe(0, 7)
+        warm_pe(0, 8)
+        warm_pe(0, 9)
+        widen(0, 1, "v")
+        warm_pe(0, 10)
+        widen(0, 2, "v")
         widen(0, 3, "v")
+        x_tp(0, 0)
+        y_tp(0, 0)
+        y_ev(0, 0, "s")
+        y_tp(0, 1)
         x_ev(0, 0, "v")
-        quant_x(0, 0)
-        y_tp(1, 0)
-        widen(1, 1, "v")
-        y_tp(1, 1)
-        quant_y(0, 0)
         y_ev(0, 1, "s")
-        y_ev(1, 0, "v")
-        quant_y(0, 1)
-        x_tp(0, 1)
-        yg_mul(0, 0)
-        square(0, 0)
-        yg_mul(0, 1)
+        widen(1, 1, "v")
+        y_tp(1, 0)
+        widen(1, 2, "v")
+        warm_pe(0, 11)
+        quant_y(0, 0)
         x_tp(1, 0)
-        square(0, 1)
+        x_tp(0, 1)
+        y_ev(1, 0, "v")
+        y_tp(1, 1)
         v_mm(0, 0)
+        quant_y(0, 1)
+        square(0, 0)
         yg_mul(1, 0)
-        quant_yg(0, 0)
-        x_ev(0, 1, "s")
+        square(0, 1)
+        yg_mul(0, 0)
         v_mm(0, 1)
+        yg_mul(0, 1)
+        x_ev(0, 1, "s")
+        quant_yg(0, 0)
+        quant_x(0, 0)
+        y_ev(1, 1, "s")
         v_mm(0, 2)
         v_mm(0, 3)
-        y_ev(1, 1, "s")
-        widen(1, 2, "v")
-        x_ev(1, 0, "v")
-        sq_mm(0, 0)
         v_sc(0, 0)
-        quant_yg(0, 1)
         v_sc(0, 1)
         v_sc(0, 2)
-        quant_y(1, 0)
-        quant_yg(1, 0)
-        v_sc(0, 3)
+        x_ev(1, 0, "v")
         quant_x(0, 1)
-        sq_mm(0, 1)
+        v_sc(0, 3)
+        sq_mm(0, 0)
+        quant_yg(1, 0)
         yg_mul(1, 1)
-        gram(0, 0)
-        gram(0, 1)
-        gram(0, 2)
+        quant_yg(0, 1)
+        square(1, 0)
+        sq_mm(0, 1)
         widen(1, 3, "s")
-        gram(0, 3)
-        quant_y(1, 1)
-        quant_x(1, 0)
-        gp_tp()
-        x_tp(1, 1)
+        quant_y(1, 0)
+        quant_yg(1, 1)
         v_inter(0, 0)
         v_inter(0, 1)
         quant_v(0, 0)
-        square(1, 0)
         quant_v(0, 1)
         sq_copy(0)
-        sq_mm(1, 0)
-        square(1, 1)
-        gp_ev()
-        quant_yg(1, 1)
+        gram(0, 0)
+        quant_y(1, 1)
+        quant_x(1, 0)
         logit(0, 0)
+        gram(0, 1)
+        gram(0, 2)
+        x_tp(1, 1)
         logit(0, 1)
+        square(1, 1)
         rmin(0, 0)
-        v_mm(1, 0)
-        sq_mm(1, 1)
+        gp_tp()
         logit(0, 2)
-        x_ev(1, 1, "s")
-        v_mm(1, 1)
-        exp(0, 0)
         rmin(0, 1)
+        exp(0, 0)
+        rmin(0, 2)
+        gram(0, 3)
+        gp_ev()
+        recip(0, 0)
         exp(0, 1)
         logit(0, 3)
-        recip(0, 0)
-        rmin(0, 2)
-        v_mm(1, 2)
-        rmin(0, 3)
-        v_sc(1, 0)
+        sq_mm(1, 0)
+        sq_mm(1, 1)
         exp(0, 2)
-        recip(0, 1)
-        exp(0, 3)
+        x_ev(1, 1, "s")
         pg_mul(0, 0)
+        recip(0, 1)
+        v_mm(1, 0)
+        sq_copy(1)
+        pg_tp(0, 0)
+        rmin(0, 3)
         gram(1, 0)
         gram(1, 1)
-        quant_x(1, 1)
         recip(0, 2)
-        sq_copy(1)
-        v_sc(1, 1)
+        pg_ev(0, 0, "s")
         pg_mul(0, 1)
-        v_sc(1, 2)
         pg_mul(0, 2)
-        pg_tp(0, 0)
-        recip(0, 3)
-        pg_tp(0, 1)
-        gram(1, 2)
+        v_sc(1, 0)
+        quant_x(1, 1)
+        exp(0, 3)
+        v_mm(1, 1)
         logit(1, 0)
-        gram(1, 3)
+        quant_pg(0, 0)
         logit(1, 1)
+        pg_tp(0, 1)
+        pg_ev(0, 1, "s")
         rmin(1, 0)
         rmin(1, 1)
+        v_sc(1, 1)
+        v_mm(1, 2)
+        gram(1, 2)
+        v_sc(1, 2)
         logit(1, 2)
-        pg_ev(0, 0, "s")
-        pg_ev(0, 1, "s")
-        pg_tp(0, 2)
-        quant_pg(0, 0)
-        v_mm(1, 3)
-        exp(1, 0)
-        u_mx(0, 0)
-        v_sc(1, 3)
+        gram(1, 3)
         logit(1, 3)
-        u_mx(0, 1)
-        rmin(1, 2)
-        recip(1, 0)
+        exp(1, 0)
         exp(1, 1)
-        rmin(1, 3)
-        pg_ev(0, 2, "s")
-        quant_pg(0, 1)
-        exp(1, 2)
+        recip(1, 0)
+        v_mm(1, 3)
+        rmin(1, 2)
         recip(1, 1)
-        pg_mul(0, 3)
-        u_mp(0, 0)
+        u_mx(0, 0)
+        rmin(1, 3)
+        pg_tp(0, 2)
+        u_mx(0, 1)
         pg_mul(1, 0)
-        recip(1, 2)
-        exp(1, 3)
+        quant_pg(0, 1)
+        v_sc(1, 3)
+        pg_ev(0, 2, "s")
+        recip(0, 3)
+        u_mp(0, 0)
         pg_mul(1, 1)
+        exp(1, 2)
         u_mx(0, 2)
-        u_mx(1, 0)
-        pg_tp(1, 0)
         u_mp(0, 1)
+        recip(1, 2)
+        pg_tp(1, 0)
+        u_mx(1, 0)
+        exp(1, 3)
+        gelu_warm()
         pg_tp(1, 1)
         finish(0, 0)
-        pg_mul(1, 2)
         v_inter(1, 0)
+        quant_pg(0, 2)
+        pg_mul(0, 3)
+        pg_mul(1, 2)
         pg_ev(1, 0, "s")
         v_inter(1, 1)
         pg_ev(1, 1, "s")
-        finish(0, 1)
-        quant_pg(0, 2)
-        quant_v(1, 0)
         pg_tp(0, 3)
-        pg_tp(1, 2)
-        quant_pg(1, 0)
+        finish(0, 1)
         pg_ev(0, 3, "s")
+        u_mp(0, 2)
+        quant_v(1, 0)
+        pg_tp(1, 2)
         recip(1, 3)
-        u_mx(1, 1)
+        quant_pg(1, 0)
         quant_v(1, 1)
         pg_ev(1, 2, "s")
-        quant_pg(1, 1)
-        u_mp(0, 2)
-        u_mx(1, 2)
-        pg_mul(1, 3)
-        gelu_warm()
+        u_mx(1, 1)
+        u_mx(0, 3)
         u_mp(1, 0)
+        finish(0, 2)
+        finish(1, 0)
+        quant_pg(1, 1)
+        pg_mul(1, 3)
+        quant_pg(0, 3)
         u_mp(1, 1)
         pg_tp(1, 3)
         quant_pg(1, 2)
-        quant_pg(0, 3)
-        pg_ev(1, 3, "v")
-        finish(0, 2)
-        u_mp(1, 2)
-        u_mx(0, 3)
-        quant_pg(1, 3)
-        finish(1, 0)
         u_mp(0, 3)
-        u_mx(1, 3)
         finish(1, 1)
-        finish(1, 2)
+        u_mx(1, 2)
+        u_mp(1, 2)
         finish(0, 3)
+        pg_ev(1, 3, "v")
+        u_mx(1, 3)
+        quant_pg(1, 3)
         u_mp(1, 3)
+        finish(1, 2)
         finish(1, 3)

from contextlib import ExitStack

import concourse.mybir as mybir
from concourse.masks import make_identity

B, N, M, D, F = 2, 512, 512, 512, 512
FLOPS = 4 * 2 * B * 512 * 512 * 512

F32 = mybir.dt.float32
BF16 = mybir.dt.bfloat16
U32 = mybir.dt.uint32
I32 = mybir.dt.int32
U8 = mybir.dt.uint8
E4M3 = mybir.dt.float8_e4m3fn
E4M3X4 = mybir.dt.float8_e4m3fn_x4
E2M1X4 = mybir.dt.float4_e2m1fn_x4
ACT = mybir.ActivationFunctionType
ALU = mybir.AluOpType
AX = mybir.AxisListType

P = 128
RSD = 512 ** -0.5


def tile_visiongnnsoftgrapher_d1p_kernel(
    tc, x_bytes, x_scale, y, g, gp, gv, wr_words, wr_scales, wm_words, wm_scales, out
):
    nc = tc.nc
    with ExitStack() as ctx:
        pool = ctx.enter_context(tc.tile_pool(name="sb", bufs=1))
        psum = ctx.enter_context(tc.psum_pool(name="ps", bufs=1))
        ctx.enter_context(tc.manual_schedule())

        def sb(name, shape, dt):
            return pool.tile(shape, dt, name=name, tag=name, bufs=1, align_bytes=64)

        def bank(tag, bufs):
            return psum.tile([P, 512], F32, name=tag, tag=tag, bufs=bufs)

        def tbank():
            return bank("tp", 3)

        def mbank():
            return bank("mm", 4)

        xs = sb("xs", [P, B, 16], F32)
        nc.sync.dma_start(out=xs[:], in_=x_scale.rearrange("b (p i) q -> p b (i q)", i=4))
        x8 = [sb("x8_%d" % b, [P, 2048], U8) for b in range(B)]
        ysb = [[sb("y_%d_%d" % (b, v), [P, 2, 512], BF16) for v in range(2)] for b in range(B)]
        y_v = [y[b].rearrange("(p t) d -> p t d", t=4) for b in range(B)]
        x_v = [x_bytes[b].rearrange("(p i) d -> p (i d)", i=4) for b in range(B)]
        small = {}

        def load_small(nm, src):
            small[nm] = sb("s_" + nm, [P, 4], BF16)
            nc.sync.dma_start(out=small[nm][:], in_=src.rearrange("(p t) -> p t", t=4))

        def load_y(b, v):
            nc.sync.dma_start(out=ysb[b][v][:], in_=y_v[b][:, 2 * v : 2 * v + 2, :])

        wq = {}
        ws = {}
        for nm in ("wm", "wr"):
            wq[nm] = sb("w_" + nm, [P, 1024], U8)
            ws[nm] = sb("ws_" + nm, [P, 512], U8)
            nc.vector.memset(ws[nm][:].bitcast(I32), 0)

        def load_w(nm, w, s):
            nc.sync.dma_start(out=wq[nm][:], in_=w[0])
            for q in range(4):
                nc.sync.dma_start(
                    out=ws[nm][32 * q : 32 * q + 4, :].bitcast(I32), in_=s[0, 4 * q : 4 * q + 4, :].bitcast(I32)
                )

        nc.sync.dma_start(out=x8[0][:, 0:1024], in_=x_v[0][:, 0:1024])
        nc.sync.dma_start(out=x8[0][:, 1024:2048], in_=x_v[0][:, 1024:2048])
        load_y(0, 0)
        nc.sync.dma_start(out=x8[1][:], in_=x_v[1])
        load_y(0, 1)
        load_small("g", g)
        load_y(1, 0)
        load_y(1, 1)
        load_small("gv", gv)
        load_w("wm", wm_words, wm_scales)
        load_small("gp", gp)
        load_w("wr", wr_words, wr_scales)

        zz = sb("zz", [P, P], F32)
        nc.vector.memset(zz[:], 0.0)
        wps = bank("sq", 1)

        def warm_pe(b, k):
            nc.tensor.matmul(wps[:, 0:128], lhsT=zz[:], rhs=zz[:], start=True, stop=True)

        ident = sb("ident", [P, P], F32)
        make_identity(nc, ident[:])
        warm = sb("warm", [P, 2], F32)
        nc.vector.memset(warm[:], 0.0)
        nc.scalar.activation(out=warm[:, 1:2], in_=warm[:, 0:1], func=ACT.Exp)
        gl = sb("gl", [P, 4, P], F32)
        nc.gpsimd.tensor_copy(out=gl[:], in_=small["g"][:].unsqueeze(2).to_broadcast([P, 4, P]))
        gv32 = sb("gv32", [P, 4], F32)
        nc.gpsimd.tensor_copy(out=gv32[:], in_=small["gv"][:])
        gp32 = sb("gp32", [P, 4], F32)
        nc.gpsimd.tensor_copy(out=gp32[:], in_=small["gp"][:])

        xb = [sb("xb_%d" % b, [P, 4, 512], BF16) for b in range(B)]
        xT = [sb("xT_%d" % b, [P, 512, 4], BF16) for b in range(B)]
        yT = [sb("yT_%d" % b, [P, 4, P, 4], BF16) for b in range(B)]
        ygT = [sb("ygT_%d" % b, [P, 2, P, 2, 4], BF16) for b in range(B)]
        y2 = [sb("y2_%d" % b, [P, 4, 2, P, 2], F32) for b in range(B)]
        sqs = [sb("sqs_%d" % b, [P, 512], F32) for b in range(B)]
        gpb = sb("gpb", [P, 2, P, 2], BF16)
        vb = [sb("vb_%d" % b, [P, 4, 512], BF16) for b in range(B)]
        vT = [sb("vT_%d" % b, [P, 512, 4], BF16) for b in range(B)]
        codes = {}
        for nm in ("x", "y", "yg", "v", "pg"):
            for b in range(B):
                codes[nm, b] = (sb("c_%s_%d" % (nm, b), [P, 512], U32), sb("k_%s_%d" % (nm, b), [P, 512], U8))

        def quant(nm, b, lo, hi, flat):
            c, k = codes[nm, b]
            nc.vector.quantize_mx(out=c[:, lo:hi].bitcast(E4M3X4), scales=k[:, lo:hi], in_=flat)

        def widen(b, i, eng):
            for q in range(4):
                o = xb[b][:, i, 128 * q : 128 * q + 128]
                s = xs[:, b, 4 * i + q : 4 * i + q + 1]
                src8 = x8[b][:, 512 * i + 128 * q : 512 * i + 128 * q + 128].bitcast(E4M3)
                if eng == "v":
                    nc.vector.tensor_scalar(out=o, in0=src8, scalar1=s, scalar2=None, op0=ALU.mult)
                else:
                    nc.scalar.activation(out=o, in_=src8, func=ACT.Copy, scale=s)

        def trans_pair(rows0, rows1):
            tb = tbank()
            t4 = tb[:].rearrange("p (e u r) -> p e u r", e=2, u=2)
            for e, rows in ((0, rows0), (1, rows1)):
                w = rows.bitcast(F32)
                for u in range(2):
                    nc.tensor.transpose(t4[:, e, u, :], w[:, u:256:2], ident[:])
            return t4

        def evac(eng, dst_words, t4):
            src_v = t4.rearrange("p e u r -> p e r u")
            if eng == "v":
                nc.vector.tensor_copy(out=dst_words, in_=src_v)
            else:
                nc.scalar.copy(out=dst_words, in_=src_v)

        tps = {}

        def y_tp(b, v):
            tps["y", b, v] = trans_pair(ysb[b][v][:, 0, :], ysb[b][v][:, 1, :])

        def y_ev(b, v, eng):
            dst = yT[b][:, 2 * v : 2 * v + 2, :, :].rearrange("p t r k -> p (t r k)").bitcast(F32)
            evac(eng, dst.rearrange("p (e r u) -> p e r u", e=2, u=2), tps["y", b, v])

        def x_tp(b, v):
            tps["x", b, v] = trans_pair(xb[b][:, 2 * v, :], xb[b][:, 2 * v + 1, :])

        def x_ev(b, v, eng):
            dst = xT[b][:, 256 * v : 256 * v + 256, :].rearrange("p r k -> p (r k)").bitcast(F32)
            evac(eng, dst.rearrange("p (e r u) -> p e r u", e=2, u=2), tps["x", b, v])

        def yg_mul(b, v):
            nc.vector.tensor_tensor(
                out=ygT[b][:, v],
                in0=yT[b][:, 2 * v : 2 * v + 2, :, :].rearrange("p e r k -> p r e k"),
                in1=small["g"][:].unsqueeze(1).unsqueeze(1).to_broadcast([P, P, 2, 4]),
                op=ALU.mult,
            )

        def quant_yg(b, v):
            quant("yg", b, 256 * v, 256 * v + 256, ygT[b][:, v].rearrange("p r e k -> p (r e k)"))

        def quant_y(b, v):
            quant("y", b, 256 * v, 256 * v + 256, yT[b][:, 2 * v : 2 * v + 2].rearrange("p t r k -> p (t r k)"))

        def quant_x(b, v):
            quant("x", b, 256 * v, 256 * v + 256, xT[b][:, 256 * v : 256 * v + 256].rearrange("p r k -> p (r k)"))

        def square(b, v):
            nc.scalar.activation(
                out=y2[b][:, :, v],
                in_=yT[b][:, 2 * v : 2 * v + 2, :, :].rearrange("p e r k -> p k r e"),
                func=ACT.Square,
            )

        sq_ps = {}

        def sq_mm(b, v):
            if v == 0:
                sq_ps[b] = bank("sq", 1)
            for k in range(4):
                nc.tensor.matmul(
                    sq_ps[b][:, 256 * v : 256 * v + 256],
                    lhsT=gl[:, k, :],
                    rhs=y2[b][:, k, v].rearrange("p r e -> p (r e)"),
                    start=(k == 0),
                    stop=(k == 3),
                )

        def sq_copy(b):
            nc.scalar.activation(out=sqs[b][:], in_=sq_ps[b][:], func=ACT.Copy, scale=RSD)

        def mx(o, a, asl, wt, start, stop):
            ca, ka = a
            nc.tensor.matmul_mx(
                out=o,
                lhsT=ca[:, asl].bitcast(E4M3X4),
                lhsT_scale=ka[:, asl],
                rhs=wt[0],
                rhs_scale=wt[1],
                start=start,
                stop=stop,
            )

        def cols(i):
            return slice(128 * i, 128 * i + 128)

        def mov(nm, b):
            c, k = codes[nm, b]
            return c[:].bitcast(E4M3X4), k[:]

        def wmov(nm, lo, n):
            return wq[nm][:, 2 * lo : 2 * lo + 2 * n].bitcast(E2M1X4), ws[nm][:, lo : lo + n]

        v_ps = {}

        def v_mm(b, t):
            v_ps[b, t] = mbank()
            mx(v_ps[b, t][:], codes["y", b], cols(t), wmov("wm", 0, 512), True, True)

        def v_sc(b, t):
            nc.scalar.activation(out=vb[b][:, t, :], in_=v_ps[b, t][:], func=ACT.Copy, scale=gv32[:, t : t + 1])

        def v_inter(b, h):
            nc.vector.tensor_copy(
                out=vT[b][:, 256 * h : 256 * h + 256, :], in_=vb[b][:, :, 256 * h : 256 * h + 256].rearrange("p t f -> p f t")
            )

        def v_mm4(b, c):
            v_ps[b, c] = mbank()
            for t in range(4):
                mx(v_ps[b, c][:, 128 * t : 128 * t + 128], codes["y", b], cols(t), wmov("wm", 128 * c, 128), True, True)

        def v_mul(b, c):
            nc.vector.tensor_tensor(
                out=vT[b][:, 128 * c : 128 * c + 128, :],
                in0=v_ps[b, c][:].rearrange("p (t f) -> p f t", t=4),
                in1=gv32[:].unsqueeze(1).to_broadcast([P, P, 4]),
                op=ALU.mult,
            )

        def quant_v(b, h):
            quant("v", b, 256 * h, 256 * h + 256, vT[b][:, 256 * h : 256 * h + 256].rearrange("p f t -> p (f t)"))

        def gp_tp():
            tps["gp"] = tbank()
            for t in range(4):
                nc.tensor.transpose(tps["gp"][:, 128 * t : 128 * t + 128], gp32[:, t : t + 1].to_broadcast([P, P]), ident[:])

        def gp_ev():
            nc.scalar.copy(out=gpb[:], in_=tps["gp"][:].rearrange("p (u e r) -> p u r e", u=2, e=2))

        nl = {}
        ex = {}
        mn = {}
        zs = {}
        rz = {}
        gram_ps = {}

        def gram(b, i):
            ps = mbank()
            mx(ps[:], codes["x", b], cols(i), mov("yg", b), True, True)
            gram_ps[b, i] = ps

        def logit(b, i):
            nl[b, i] = sb("nl_%d_%d" % (b, i), [P, 512], F32)
            nc.vector.scalar_tensor_tensor(
                out=nl[b, i][:], in0=gram_ps[b, i][:], scalar=-2.0 * RSD, in1=sqs[b][:], op0=ALU.mult, op1=ALU.add
            )

        def rmin(b, i):
            mn[b, i] = sb("mn_%d_%d" % (b, i), [P, 1], F32)
            nc.vector.tensor_reduce(out=mn[b, i][:], in_=nl[b, i][:], axis=AX.X, op=ALU.min)

        def exp(b, i):
            ex[b, i] = sb("ex_%d_%d" % (b, i), [P, 512], F32)
            zs[b, i] = sb("zs_%d_%d" % (b, i), [P, 1], F32)
            nc.scalar.activation(
                out=ex[b, i][:], in_=nl[b, i][:], func=ACT.Exp, bias=mn[b, i][:], scale=-1.0, accum_out=zs[b, i][:]
            )

        def recip(b, i):
            rz[b, i] = sb("rz_%d_%d" % (b, i), [P, 1], F32)
            nc.vector.reciprocal(out=rz[b, i][:], in_=zs[b, i][:])

        pgs = {}

        def pg_mul(b, i):
            pgs[b, i] = sb("pg_%d_%d" % (b, i), [P, 512], BF16)
            nc.vector.scalar_tensor_tensor(
                out=pgs[b, i][:],
                in0=ex[b, i][:],
                scalar=rz[b, i][:],
                in1=gpb[:].rearrange("p u r e -> p (u r e)"),
                op0=ALU.mult,
                op1=ALU.mult,
            )

        pgT = {}

        def pg_tp(b, i):
            tb = tbank()
            tps["pg", b, i] = tb
            w = pgs[b, i][:].bitcast(F32)
            for u in range(2):
                nc.tensor.transpose(tb[:, 128 * u : 128 * u + 128], w[:, 128 * u : 128 * u + 128], ident[:])

        def pg_ev(b, i, eng):
            pgT[b, i] = sb("pgT_%d_%d" % (b, i), [P, 512], BF16)
            dst = pgT[b, i][:].bitcast(F32).rearrange("p (r u) -> p r u", u=2)
            src_v = tps["pg", b, i][:, 0:256].rearrange("p (u r) -> p r u", u=2)
            if eng == "v":
                nc.vector.tensor_copy(out=dst, in_=src_v)
            else:
                nc.scalar.copy(out=dst, in_=src_v)

        def quant_pg(b, i):
            quant("pg", b, 128 * i, 128 * i + 128, pgT[b, i][:])

        u_ps = {}

        def u_mx(b, i):
            u_ps[b, i] = mbank()
            mx(u_ps[b, i][:], codes["x", b], cols(i), wmov("wr", 0, 512), True, False)

        def u_mp(b, i):
            mx(u_ps[b, i][:], codes["pg", b], cols(i), mov("v", b), False, True)

        def gelu_warm():
            nc.scalar.activation(out=warm[:, 1:2], in_=warm[:, 0:1], func=ACT.Gelu)

        o_v = [out[b].rearrange("(p i) f -> p i f", i=4) for b in range(B)]

        def finish(b, i):
            o = sb("o_%d_%d" % (b, i), [P, 512], F32)
            parts = 2 if (b, i) == (B - 1, 3) else 1
            w = 512 // parts
            for h in range(parts):
                nc.scalar.activation(out=o[:, h * w : h * w + w], in_=u_ps[b, i][:, h * w : h * w + w], func=ACT.Gelu)
                nc.sync.dma_start(out=o_v[b][:, i, h * w : h * w + w], in_=o[:, h * w : h * w + w])

        warm_pe(0, 0)
        warm_pe(0, 1)
        warm_pe(0, 2)
        widen(1, 0, "s")
        warm_pe(0, 3)
        warm_pe(0, 4)
        warm_pe(0, 5)
        widen(0, 0, "v")
        warm_pe(0, 6)
        warm_pe(0, 7)
        warm_pe(0, 8)
        warm_pe(0, 9)
        widen(0, 1, "v")
        warm_pe(0, 10)
        widen(0, 2, "v")
        widen(0, 3, "v")
        x_tp(0, 0)
        y_tp(0, 0)
        y_ev(0, 0, "s")
        y_tp(0, 1)
        x_ev(0, 0, "v")
        y_ev(0, 1, "s")
        widen(1, 1, "v")
        y_tp(1, 0)
        widen(1, 2, "v")
        warm_pe(0, 11)
        quant_y(0, 0)
        x_tp(1, 0)
        x_tp(0, 1)
        y_ev(1, 0, "v")
        y_tp(1, 1)
        v_mm(0, 0)
        quant_y(0, 1)
        square(0, 0)
        yg_mul(1, 0)
        square(0, 1)
        yg_mul(0, 0)
        v_mm(0, 1)
        yg_mul(0, 1)
        x_ev(0, 1, "s")
        quant_yg(0, 0)
        quant_x(0, 0)
        y_ev(1, 1, "s")
        v_mm(0, 2)
        v_mm(0, 3)
        v_sc(0, 0)
        v_sc(0, 1)
        v_sc(0, 2)
        x_ev(1, 0, "v")
        quant_x(0, 1)
        v_sc(0, 3)
        sq_mm(0, 0)
        quant_yg(1, 0)
        yg_mul(1, 1)
        quant_yg(0, 1)
        square(1, 0)
        sq_mm(0, 1)
        widen(1, 3, "s")
        quant_y(1, 0)
        quant_yg(1, 1)
        v_inter(0, 0)
        v_inter(0, 1)
        quant_v(0, 0)
        quant_v(0, 1)
        sq_copy(0)
        gram(0, 0)
        quant_y(1, 1)
        quant_x(1, 0)
        logit(0, 0)
        gram(0, 1)
        gram(0, 2)
        x_tp(1, 1)
        logit(0, 1)
        square(1, 1)
        rmin(0, 0)
        gp_tp()
        logit(0, 2)
        rmin(0, 1)
        exp(0, 0)
        rmin(0, 2)
        gram(0, 3)
        gp_ev()
        recip(0, 0)
        exp(0, 1)
        logit(0, 3)
        sq_mm(1, 0)
        sq_mm(1, 1)
        exp(0, 2)
        x_ev(1, 1, "s")
        pg_mul(0, 0)
        recip(0, 1)
        v_mm(1, 0)
        sq_copy(1)
        pg_tp(0, 0)
        rmin(0, 3)
        gram(1, 0)
        gram(1, 1)
        recip(0, 2)
        pg_ev(0, 0, "s")
        pg_mul(0, 1)
        pg_mul(0, 2)
        v_sc(1, 0)
        quant_x(1, 1)
        exp(0, 3)
        v_mm(1, 1)
        logit(1, 0)
        quant_pg(0, 0)
        logit(1, 1)
        pg_tp(0, 1)
        pg_ev(0, 1, "s")
        rmin(1, 0)
        rmin(1, 1)
        v_sc(1, 1)
        v_mm(1, 2)
        gram(1, 2)
        v_sc(1, 2)
        logit(1, 2)
        gram(1, 3)
        logit(1, 3)
        exp(1, 0)
        exp(1, 1)
        recip(1, 0)
        v_mm(1, 3)
        rmin(1, 2)
        recip(1, 1)
        u_mx(0, 0)
        rmin(1, 3)
        pg_tp(0, 2)
        u_mx(0, 1)
        pg_mul(1, 0)
        quant_pg(0, 1)
        v_sc(1, 3)
        pg_ev(0, 2, "s")
        recip(0, 3)
        u_mp(0, 0)
        pg_mul(1, 1)
        exp(1, 2)
        u_mx(0, 2)
        u_mp(0, 1)
        recip(1, 2)
        pg_tp(1, 0)
        u_mx(1, 0)
        exp(1, 3)
        gelu_warm()
        pg_tp(1, 1)
        finish(0, 0)
        v_inter(1, 0)
        quant_pg(0, 2)
        pg_mul(0, 3)
        pg_mul(1, 2)
        pg_ev(1, 0, "s")
        v_inter(1, 1)
        pg_ev(1, 1, "s")
        pg_tp(0, 3)
        finish(0, 1)
        pg_ev(0, 3, "s")
        u_mp(0, 2)
        quant_v(1, 0)
        pg_tp(1, 2)
        recip(1, 3)
        quant_pg(1, 0)
        quant_v(1, 1)
        pg_ev(1, 2, "s")
        u_mx(1, 1)
        u_mx(0, 3)
        u_mp(1, 0)
        finish(0, 2)
        finish(1, 0)
        quant_pg(1, 1)
        pg_mul(1, 3)
        quant_pg(0, 3)
        u_mp(1, 1)
        pg_tp(1, 3)
        quant_pg(1, 2)
        u_mp(0, 3)
        finish(1, 1)
        u_mx(1, 2)
        u_mp(1, 2)
        finish(0, 3)
        pg_ev(1, 3, "v")
        u_mx(1, 3)
        quant_pg(1, 3)
        u_mp(1, 3)
        finish(1, 2)
        finish(1, 3)
